import numpy as np, ml_dtypes
CORES = [3,7,11,15,131,135,139,143]
N = 8
import mx_ref
BF = ml_dtypes.bfloat16
def tile(rs):
    return np.stack(rs, axis=2).reshape(128, -1).astype(BF)
def pick(q, e):
    c = np.concatenate([q[0].reshape(128, -1, 4), np.zeros((128, 1, 4), np.uint8)], axis=1); s = np.concatenate([q[1], np.ones((16, 1), np.uint8)], axis=1)
    return (np.ascontiguousarray(c[:, e].reshape(128, -1)), np.ascontiguousarray(s[:, e]))
def join(*qs):
    return (np.concatenate([q[0] for q in qs], axis=1), np.concatenate([q[1] for q in qs], axis=1))
def put(q, e, v):
    c, s = q[0].reshape(128, -1, 4).copy(), q[1].copy(); c[:, e] = v[0].reshape(128, -1, 4); s[:, e] = v[1]
    return (c.reshape(128, -1), s)
def pk(c, s):
    return (np.ascontiguousarray(c), mx_ref.live(s))
def emit(q):
    return q[0], q[1]
def packed(v, rng):
    q = [mx_ref.quantize(np.ascontiguousarray(v[r])) for r in range(N)]
    return np.stack([a for a, b in q]), np.stack([mx_ref.plane(b, rng) for a, b in q])
def values_of_codes():
    e, c = np.zeros((128, 128, 4), np.float32), np.zeros((128, 2, 4), np.uint8)
    e[np.arange(128), np.arange(128), 0] = 1
    c[:127, :, 0] = np.arange(256).reshape(2, 128).T[:127]
    return mx_ref.matmul(mx_ref.quantize(e.reshape(128, 512).astype(BF)), (c.reshape(128, 8), np.full((16, 2), 127, np.uint8))).T.reshape(-1).astype(np.float64)
CODE_VALUE, SCALE_VALUE = values_of_codes(), 2.0 ** (np.arange(256) - 127.0)
def decode(q):
    return (CODE_VALUE[q[0]].reshape(16, 8, -1, 4) * SCALE_VALUE[q[1]][:, None, :, None] + 0.0).reshape(128, -1).astype(np.float32)
def f(rng, *shape):
    return mx_ref.flush((rng.standard_normal(shape, dtype=np.float32) * np.exp2(rng.integers(-2, 3, shape[:-1] + (1,)))).astype(BF))
def wide(rng, *shape, cols=0):
    v = rng.standard_normal(shape, dtype=np.float32) * np.exp2(rng.integers(-12, 13, shape)).astype(np.float32)
    if cols: v *= np.repeat(np.exp2(rng.integers(-cols, cols + 1, shape[:-2] + (1, shape[-1] // 4))) * (rng.random(shape[:-2] + (1, shape[-1] // 4)) > 0.0625), 4, axis=-1).astype(np.float32)
    return mx_ref.flush(v.astype(BF))
C, A, R = 224, 112, 3
def numbers_of(rng):
    return {"x": np.array(f(rng, N, 128, 4 * C)), "u": np.array(f(rng, N, 128, 512)), "v": np.array(f(rng, N, 128, 512))}
def layers(rng):
    return np.array(f(rng, N, 128, 2048)).reshape(N, 8, 16, 4, 8, 16, 4)
def weights(rng, w):
    c, s = packed(np.ascontiguousarray(w).reshape(N, 128, 2048), rng)
    return {"wc": c, "ws": s}
def setup_inputs(rng):
    return {**numbers_of(rng), **weights(rng, layers(rng))}
def setup_inputs_ties(rng):
    d = numbers_of(rng)
    x = d["x"].reshape(N, 8, 16, C, 4)
    u = d["u"].reshape(N, 128, 128, 4)
    e = rng.permutation(N)
    for i, r in enumerate(e):
        k = np.arange(C) % 3
        if i % 2 == 0: k = k[rng.permutation(C)]
        if i == 0: k = np.zeros(C, int)
        a = x[r][:, :8, :3].copy()
        a[:, :, 2] = 0
        x[r][:, :8] = a[:, :, k]
        if i % 4 in (0, 3):
            u[r][:, ::16] = u[r][:, :1].copy()
            u[r][:, 1::16] = u[r][:, 1:2].copy()
    x[e[1]] = 0
    h = u.reshape(N, 8, 16, 128, 4)
    h[:, :, 8:, ::16] = 0
    h[:, :, 8:, 1::16] = 0
    w = layers(rng)
    w[:, :, :, :, :, :8] = 0
    return {"x": x.reshape(N, 128, 4 * C), "u": u.reshape(N, 128, 512), "v": d["v"], **weights(rng, w)}
def setup_inputs_near(rng):
    d = numbers_of(rng)
    x = d["x"].astype(np.float32).reshape(N, 8, 16, C, 4)
    u = d["u"].reshape(N, 128, 128, 4)
    u[:, :, ::16] = 0
    u[:, :, 1::16] = 0
    x[:, :, 0] = 0
    x[:, :, 8:] = 0
    o = rng.permutation(N) % 4
    for r in range(N):
        k = 1.0 if o[r] == 0 else 2.0 ** -30
        if o[r] < 3: x[r, :, 8] = ((rng.integers(0, 16, (8, C))[:, :, None] >> np.arange(4)) & 1) * np.exp2(np.arange(4) - 23.0)
        if o[r] < 2:
            x[r, :, 0, :, 0] = rng.integers(0, 2, (8, C)) * 2.0 - 1.0
            x[r, :, 11, :, 0] = 2.0 ** -10
        if o[r] == 2:
            for g in rng.permutation(8)[:4]: x[r, g, 0, rng.integers(C), 0] = 2.0 ** 16 * rng.choice([-1.0, 1.0])
        if o[r] == 3:
            s = rng.integers(0, 2, (8, C)) * 0.125
            x[r, :, 10, :, 0] = (1.0 + s) * 2.0 ** -30
            x[r, :, 12, :, 0] = (1.125 - s) * 2.0 ** -30
        for h in range(0, 128, 16):
            for c, a in ((h, h), (h + 1, (h + 16) % 128)):
                if o[r] < 3:
                    u[r, a, c, 0] = 2.0 ** 30 if o[r] == 2 else k
                    u[r, a + 8, c] = k
                if o[r] < 2: u[r, a + 11, c, 0] = k
                if o[r] == 3:
                    u[r, a + 10, c, 0] = 1.25 * k
                    u[r, a + 12, c, 0] = 1.125 * k
    w = layers(rng)
    for i in [0] + [8 + j for j in range(8)]:
        w[:, :, i] = 0
        w[:, :, :, :, :, i] = 0
    return {"x": x.reshape(N, 128, 4 * C).astype(BF), "u": u.reshape(N, 128, 512), "v": d["v"], **weights(rng, w)}
def setup_inputs_ends(rng):
    d = numbers_of(rng)
    o = (np.arange(N) + rng.integers(N)) % 4
    x = np.zeros((N, 8, 16, C, 4), np.float32)
    u = d["u"].reshape(N, 128, 128, 4)
    for r in range(N):
        a = 2.0 ** 30 * (1.0 - 0.1 * rng.random((128, 8, 2, 4)))
        if o[r] == 0:
            x[r] = -2.0 ** 29 * (0.8 + 0.075 * rng.random((8, 16, C, 4)))
            a[:, :, 0] *= np.exp2(-1.0 * np.concatenate([rng.permutation(4), rng.permutation(4)]))[:, None]
            d["v"][r] = (2.0 ** 30 * rng.choice([-1.0, 1.0], (128, 512))).astype(np.float32).astype(BF)
        if o[r] == 1:
            x[r] = 2.0 ** 29 * np.where((rng.permutation(C) % 2 == 0)[:, None], 0.875, -0.7 - 0.07 * rng.random((8, 16, C, 4)))
            a *= rng.choice([-1.0, 1.0], (8, 2))[None, :, :, None]
        if o[r] == 2:
            x[r] = 2.0 ** -30 * rng.choice([-1.0, 1.0], (8, 16, C, 4))
            a = 2.0 ** -30 * rng.choice([-1.0, 1.0], (128, 8, 2, 4))
            a[0, :, :, 0] = 0
            d["v"][r] = (2.0 ** -30 * rng.choice([-1.0, 1.0], (128, 512))).astype(np.float32).astype(BF)
        if o[r] == 3:
            x[r] = (1.0 + rng.random((8, 16, 1, 4))) * rng.choice([-1.0, 1.0], (8, 16, 1, 4))
            a = (1.0 + rng.random((128, 1, 2, 4))) * rng.choice([-1.0, 1.0], (128, 1, 2, 4)) * np.ones((1, 8, 1, 1))
        a = a.astype(np.float32).astype(BF)
        u[r][:, ::16] = a[:, :, 0]
        u[r][:, 1::16] = a[:, :, 1]
    w = np.zeros((N, 128, 4, 128, 4), np.float32)
    i = np.arange(128)
    for b in range(4): w[:, i, b, i, b] = 2
    return {"x": x.reshape(N, 128, 4 * C).astype(BF), "u": u.reshape(N, 128, 512), "v": d["v"], **weights(rng, w.astype(BF))}
def setup_inputs_odd(rng):
    d = numbers_of(rng)
    k = (N, 8, 16, C, 4)
    x = (129.0 + 2.0 * rng.integers(0, 64, k)) * np.exp2(rng.integers(-21, -14, k)) * rng.choice([-1.0, 1.0], k)
    x[:, :, ::8] = 0
    x[:, :, ::8, :, 0] = np.where(rng.random((N, 8, 2, C)) < 0.5, 1.96875, 1.875)
    w = layers(rng)
    w[:, :, ::8] = 0
    w[:, :, :, :, :, ::8] = 0
    return {"x": x.astype(np.float32).reshape(N, 128, 4 * C).astype(BF), "u": d["u"], "v": d["v"], **weights(rng, w)}
def setup_inputs_spread(rng):
    d = setup_inputs(rng)
    d["x"] = np.clip(wide(rng, N, 128, 4 * C, cols=2).astype(np.float32), -65536.0, 65536.0).astype(BF)
    return d
def check_inputs(d):
    b = []
    for k in ("x", "u", "v"):
        a = np.abs(d[k].astype(np.float32))
        if not (np.isfinite(a).all() and ((a == 0) | (a >= 2.0 ** -30) & (a <= 2.0 ** 30)).all()): b.append("a value of " + k)
    none, least, most = [emit(mx_ref.quantize(np.full((128, 16), k, np.float32).astype(BF)))[1][0, 0] for k in (0.0, 2.0 ** -30, 2.0 ** 30)]
    total = 0.0
    for r in range(N):
        if ((d["wc"][r] == 0x7F) | (d["wc"][r] == 0xFF)).any(): b.append("wc: a code that is no number")
        s = mx_ref.live(d["ws"][r])
        if ((s != none) & ((s < least) | (s > most))).any(): b.append("ws: a scale out of range")
        w = np.abs(decode(pk(d["wc"][r], d["ws"][r])).astype(np.float64)).reshape(128, 512, 4)
        total = max(total, float(np.max(np.sum(w, axis=(0, 2)))))
    a = float(np.max(np.abs(d["x"].astype(np.float32))))
    if not a * (1.0 + total * 0.015625) ** 3 <= 2.0 ** 29: b.append("x and W: a * (1 + s)**3")
    return b
def departures(s):
    half = np.argsort(-s[::16].reshape(2, 4 * C), axis=1, kind="stable") // C
    leaf = np.argsort(-s[1::16], axis=1, kind="stable")
    e = np.zeros((8, C), np.int64)
    for g in range(8): e[g, leaf[g]] = 2 * np.flatnonzero(half[g // 4] == g % 4) + g // 4
    return e.reshape(-1)
def reference(x, u, v, wc, ws):
    qu = [mx_ref.quantize(u[r]) for r in range(N)]
    lay = [pk(wc[r], ws[r]) for r in range(N)]
    now = [x[r] for r in range(N)]
    for t in range(R):
        own, dep, sent = [], [], []
        for r in range(N):
            q = mx_ref.quantize(now[r])
            dep.append(departures(mx_ref.matmul(qu[r], q) + np.float32(0.0)))
            own.append(decode(q).reshape(8, 16, C, 4).transpose(0, 2, 1, 3).reshape(8 * C, 16, 4))
            p = own[r][np.argsort(dep[r])]
            e = ((p[:4 * C] + p[4 * C:]) * np.float32(0.5)).astype(BF)
            sent.append(mx_ref.quantize(np.ascontiguousarray(e.reshape(A, 8, 16, 4).transpose(1, 2, 0, 3)).reshape(128, 4 * A)))
        for r in range(N):
            q = sent[r - 1]
            h = tile([mx_ref.matmul(pick(lay[r], np.arange(128 * b, 128 * b + 128)), q) * np.float32(0.015625) for b in range(4)])
            h = h.reshape(8, 16, A, 4).transpose(2, 0, 1, 3).reshape(8 * A, 16, 4).astype(np.float32)
            z = (own[r] + h[dep[r] % (4 * C)]).astype(BF)
            now[r] = np.ascontiguousarray(z.reshape(8, C, 16, 4).transpose(0, 2, 1, 3)).reshape(128, 4 * C)
    y, op = np.zeros((N, 128, C), np.float32), np.zeros((N, 8, C), np.float32)
    oc, osc = np.zeros((N, 128, 4 * C), np.uint8), np.zeros((N, 16, C), np.uint8)
    for r in range(N):
        q = mx_ref.quantize(now[r])
        y[r] = mx_ref.matmul(mx_ref.quantize(v[r]), q)
        op[r] = dep[r].reshape(8, C)
        oc[r], osc[r] = emit(q)
    return {"y": y, "op": op, "oc": oc, "osc": osc}

@@ -1,0 +1,437 @@
+from concourse.bass import IndirectOffsetOnAxis
+from concourse.mybir import dt, AluOpType, ActivationFunctionType
+
+A, AF = AluOpType, ActivationFunctionType
+C, K, R = 224, 112, 3
+NS = 4
+BIG = 1e25
+F8, U8 = "float8_e4m3fn_x4", "uint8"
+SCRATCH = {}
+
+
+def _b(name, cols, dtype="float32", where="sbuf"):
+    SCRATCH[name] = (where, [128, cols], dtype)
+
+
+for _n, _c in (("bf", 8), ("cn", 16), ("jm", C), ("dif", C), ("wz", C), ("dz", C), ("dm", C), ("tm", C), ("tn", C), ("lc", C), ("hn", 32), ("rm", 512),
+               ("z1", C), ("z0", C), ("ab", 16), ("wm", 48), ("lm", 48), ("scl", C), ("lw", 256), ("lt", 1024), ("r0s", C), ("p0s", C), ("win", 896),
+               ("sc", 896), ("v56", 56), ("pl", C), ("sce", C), ("tw", 256), ("pr", C), ("scx", C), ("opb", C), ("yb", C)):
+    _b(_n, _c)
+for _n, _c in (("ii", 2), ("bi", 8), ("ui", 40), ("wi", 128), ("hb", 2), ("px", 16), ("pa", 16), ("pb", 16), ("pg", 16)):
+    _b(_n, _c, "int32")
+for _n, _c in (("uo", 40), ("wo", 128), ("l1", 16), ("l0", 16), ("lp", 16), ("ei", 16), ("eo", 16), ("xo", 16)):
+    _b(_n, _c, "uint16")
+for _n, _c in (("xt", 896), ("ut", 512), ("vt", 512), ("on", 128), ("mb", 640), ("bb", 2568), ("bm", 512), ("kt", 2560), ("nz", 32), ("ad", 896),
+               ("ct", 19 * 896), ("sg", 4 * C), ("fw", 3584), ("fn", 896), ("qd", 680), ("g1", 448), ("et", 512), ("hw", 1792), ("zt", 512)):
+    _b(_n, _c, "bfloat16")
+for _n, _c in [("qx", C), ("qu", 128), ("up", 640), ("qv", 128), ("cd", 2560), ("ck", 640), ("ca", C), ("qc", 19 * C), ("qq", 170), ("wa", 512),
+               ("wp", 2048), ("zq", 128)] + [(n + str(r), c) for r in range(R) for n, c in (("qe", 128), ("lq", 128))]:
+    _b(_n, _c, F8)
+    _b(_n + "s", _c, U8)
+_b("ps", 4096, "float32", "psum")
+SCRATCH["ld"] = ("dram", [2, 1024], "float32")
+SEMAPHORES = ["sv", "st", "ss", "sg", "dx", "du", "dv", "dw", "dz", "doc", "dos", "dop", "dy"] + [n + str(r) for r in range(R) for n in ("ld", "lt", "snt", "arr")]
+
+
+def rank_program(g, core, T, topo):
+    rank = T.rank_of(core)
+    if rank is None:
+        return
+    nxt = T.cores[(rank + 1) % len(T.cores)]
+    Q = {"v": g.vector, "t": g.tensor, "s": g.scalar, "g": g, "y": g.sync}
+    ENG = {"v": "sv", "t": "st", "s": "ss", "g": "sg"}
+    total, known, acc = {}, {q: {} for q in Q}, {}
+
+    def cols(name, lo, hi, step=1):
+        return (T[name][:, lo:hi:step], name, lo, hi, step)
+
+    def clash(a, lo, hi, step, psum):
+        if psum:
+            return a[2] // 512 == lo // 512
+        return a[2] < hi and lo < a[3] and not (step > 1 and a[4] == step and (a[2] - lo) % step)
+
+    def wait(q, sem, val):
+        if known[q].get(sem, 0) < val:
+            Q[q].wait_ge(T.sem[sem], val)
+            known[q][sem] = val
+
+    def run(q, emit, reads, writes, sem=None, inc=1):
+        s = sem or ENG[q]
+        need = {}
+        for w, views in ((False, reads), (True, writes)):
+            for _, name, lo, hi, step in views:
+                psum = name == "ps"
+                for a in acc.get(name, []):
+                    if not clash(a, lo, hi, step, psum):
+                        continue
+                    if a[1] == s and (psum or sem is not None):
+                        continue
+                    if not psum and not (w or a[0]):
+                        continue
+                    need[a[1]] = max(need.get(a[1], 0), a[5] if a[5] else total[a[1]])
+        for k in need:
+            wait(q, k, need[k])
+        ins = emit()
+        if inc:
+            ins.then_inc(T.sem[s], inc)
+            total[s] = total.get(s, 0) + inc
+        at = total[s] if sem is None else 0
+        for w, views in ((False, reads), (True, writes)):
+            for _, name, lo, hi, step in views:
+                L = acc.setdefault(name, [])
+                if name == "ps":
+                    L[:] = [a for a in L if a[2] // 512 != lo // 512 or (not w and a[1] != s)]
+                else:
+                    L[:] = [a for a in L if not ((w or (a[1] == s and not a[0])) and lo <= a[2] and a[3] <= hi
+                                                 and (step == 1 or (a[4] == step and (a[2] - lo) % step == 0)))]
+                L.append((w, s, lo, hi, step, at))
+
+    V, S = g.vector, g.scalar
+
+    def ind(win, off):
+        return win[0].indirect(off[0])
+
+    def ts(out, in0, s1, s2, op0, op1=None):
+        rd = [in0] + [x for x in (s1, s2) if isinstance(x, tuple)]
+        a1 = s1[0] if isinstance(s1, tuple) else s1
+        a2 = s2[0] if isinstance(s2, tuple) else s2
+        if op1 is None:
+            run("v", lambda: V.tensor_scalar(out[0], in0[0], a1, a2, op0), rd, [out])
+        else:
+            run("v", lambda: V.tensor_scalar(out[0], in0[0], a1, a2, op0, op1), rd, [out])
+
+    def tt(out, a, b, op):
+        run("v", lambda: V.tensor_tensor(out[0], a[0], b[0], op), [a, b], [out])
+
+    def cp(out, a):
+        run("v", lambda: V.tensor_copy(out[0], a[0]), [a], [out])
+
+    def fill(out, c):
+        run("v", lambda: V.memset(out[0], c), [], [out])
+
+    def scan(out, d0, d1, init, o0, o1):
+        run("v", lambda: V.tensor_tensor_scan(out[0], d0[0], d1[0], init, o0, o1), [d0, d1], [out])
+
+    def gat(out, win, off):
+        run("v", lambda: V.tensor_copy(out[0], ind(win, off)), [win, off], [out])
+
+    def gadd(out, win, off, a):
+        run("v", lambda: V.tensor_tensor(out[0], ind(win, off), a[0], A.add), [win, off, a], [out])
+
+    def sca(win, off, a):
+        run("v", lambda: V.tensor_copy(ind(win, off), a[0]), [off, a], [win])
+
+    def codes(out, win, off):
+        run("v", lambda: V.tensor_copy(out[0].bitcast(dt.uint32), win[0].bitcast(dt.uint32).indirect(off[0])), [win, off], [out])
+
+    def act(out, a, func, bias=None, scale=None):
+        kw = {}
+        if bias is not None:
+            kw["bias"] = bias[0] if isinstance(bias, tuple) else bias
+        if scale is not None:
+            kw["scale"] = scale[0] if isinstance(scale, tuple) else scale
+        rd = [a] + [x for x in (bias, scale) if isinstance(x, tuple)]
+        run("s", lambda: S.activation(out[0], a[0], func, **kw), rd, [out])
+
+    def sgat(out, win, off):
+        run("s", lambda: S.activation(out[0], ind(win, off), AF.Copy), [win, off], [out])
+
+    def zeros(out):
+        n = (out[3] - out[2] + out[4] - 1) // out[4]
+        act(out, cols("rm", 0, n), AF.Copy, scale=0.0)
+
+    def quant(name, lo, hi, src, slo):
+        o, p, i = cols(name, lo, hi), cols(name + "s", lo, hi), cols(src, slo, slo + 4 * (hi - lo))
+        run("v", lambda: V.quantize_mx(o[0], p[0], i[0]), [i], [o, p])
+
+    def mm(bank, n, ln, la, rn, ra, start=True, stop=True):
+        o = cols("ps", 512 * bank, 512 * bank + n)
+        a, b = cols(ln, la, la + 128), cols(ln + "s", la, la + 128)
+        c, d = cols(rn, ra, ra + n), cols(rn + "s", ra, ra + n)
+        run("t", lambda: g.tensor.matmul_mx(o[0], a[0], b[0], c[0], d[0], start, stop), [a, b, c, d], [o])
+
+    def ps(bank, lo=0, hi=C):
+        return cols("ps", 512 * bank + lo, 512 * bank + hi)
+
+    def load(sem, out, src, name, hi):
+        run("y", lambda: g.sync.dma_start(out, src), [], [(None, name, 0, hi, 1)], sem, 16)
+
+    def store(sem, out, src, name, hi):
+        run("y", lambda: g.sync.dma_start(out, src), [(None, name, 0, hi, 1)], [], sem, 16)
+
+    def iota(out, pattern, base, cm, flag=True):
+        if flag:
+            run("g", lambda: g.iota(out[0], pattern, base, cm, allow_small_or_imprecise_dtypes=True), [], [out])
+        else:
+            run("g", lambda: g.iota(out[0], pattern, base, cm), [], [out])
+
+    load("du", T.ut[:, :], T.u[:, :], "ut", 512)
+    load("dx", T.xt[:, :], T.x[:, :], "xt", 896)
+    load("dw", T.wa[:, :].bitcast(dt.uint8), T.wc[:, :], "wa", 512)
+    load("dw", T.was[:, :], T.ws[:, :], "was", 512)
+    load("dv", T.vt[:, :], T.v[:, :], "vt", 512)
+
+    iota(cols("ii", 0, 1), [[0, 1]], 0, 1, False)
+    for k, (pat, base) in enumerate((([[16, 8]], 1), ([[16, 8]], 0), ([[32, 4], [-16, 2]], 16), ([[64, 2], [-32, 2], [16, 2]], 32), ([[64, 2], [-32, 2], [-16, 2]], 48))):
+        iota(cols("ui", 8 * k, 8 * k + 8), pat, base, 0, False)
+    iota(cols("jm", 0, C), [[0, 14], [1, 16]], 0, 0)
+    iota(cols("rm", 0, 128), [[16, 8], [0, 16]], 0, 0)
+    iota(cols("rm", 128, 256), [[32, 4], [-16, 2], [0, 16]], 16, 0)
+    for h in range(2):
+        iota(cols("rm", 256 + 64 * h, 320 + 64 * h), [[-32, 2], [16, 2], [0, 16]], 64 * h + 32, 0)
+        iota(cols("rm", 384 + 64 * h, 448 + 64 * h), [[-16, 4], [0, 16]], 64 * h + 48, 0)
+    fill(cols("on", 0, 128), 1.0)
+
+    def select(lo, pat, base):
+        o, i = cols("mb", lo, lo + 128), cols("on", 0, 128)
+        run("g", lambda: g.affine_select(o[0], i[0], pat, A.is_equal, 0.0, base, 1), [i], [o])
+
+    select(0, [[-1, 128]], 0)
+    for s in range(4):
+        select(128 + 128 * s, [[0, 4], [-64, 2], [-1, 16]], -16 * s)
+    iota(cols("lc", 0, C), [[1, C]], 0, 0)
+    iota(cols("hn", 0, 32), [[64, 2], [0, 16]], 0, 0)
+    iota(cols("wi", 0, 128), [[32, 16], [16, 2], [0, 4]], 0, 0, False)
+
+    for k, bits in enumerate((15, 112, 16, 32, 64, 48)):
+        ts(cols("bi", k, k + 1), cols("ii", 0, 1), bits, None, A.bitwise_and)
+    cp(cols("bf", 0, 6), cols("bi", 0, 6))
+    cp(cols("uo", 0, 40), cols("ui", 0, 40))
+    pi, p16, b0, b1, p64, p48 = [cols("bf", k, k + 1) for k in range(6)]
+    cn = [cols("cn", k, k + 1) for k in range(16)]
+    kp, kpm = cn[0], cn[1]
+    ts(kp, pi, 15.0, 1024.0, A.is_lt, A.mult)
+    ts(kpm, kp, 1.0, None, A.subtract)
+    dif, wz, dz, dm, jm = [cols(n, 0, C) for n in ("dif", "wz", "dz", "dm", "jm")]
+    ts(dif, jm, pi, None, A.subtract)
+    ts(wz, dif, 0.0, 2 * BIG, A.not_equal, A.mult)
+    ts(wz, wz, BIG, None, A.subtract)
+    ts(dz, jm, 0.0, 2 * BIG, A.is_equal, A.mult)
+    ts(dz, dz, BIG, None, A.subtract)
+    for k in range(5):
+        zeros(cols("bb", 512 * k, 512 * k + 512))
+    zeros(cols("bb", 2560, 2568))
+    quant("qu", 0, 128, "ut", 0)
+    for lo, hi in ((0, 16), (16, 40)):
+        codes(cols("up", 16 * lo, 16 * hi), cols("qu", 0, 128), cols("uo", lo, hi))
+        sgat(cols("ups", 16 * lo, 16 * hi), cols("qus", 0, 128), cols("uo", lo, hi))
+    act(cols("bb", 3, 3 + 2560, 4), cols("mb", 0, 640), AF.Copy)
+
+    def later_constants():
+        for k, (b, op) in enumerate(((b0, A.is_ge), (b1, A.is_ge), (b1, A.is_lt))):
+            ts(cn[2 + 2 * k], b, 1.0, 1.25 * 2.0 ** -24, op, A.mult)
+            ts(cn[3 + 2 * k], b, 1.0, 2.0 ** -120, op, A.mult)
+        for k in (3, 7):
+            zeros(cols("ct", 896 * k + 3, 896 * k + 896, 4))
+        for t in (2, 3):
+            zeros(cols("ct", 896 * 18 + t, 896 * 19, 4))
+        ts(cols("bm", 0, 512), cols("rm", 0, 512), p16, None, A.is_equal)
+        for t in range(4):
+            act(cols("kt", t, 2048, 4), cols("bm", 0, 512), AF.Copy)
+            act(cols("kt", 2048 + t, 2560, 4), cols("bm", 128 + 128 * (t // 2), 256 + 128 * (t // 2)), AF.Copy)
+
+    def decode_constants():
+        quant("ck", 0, 512, "kt", 0)
+        quant("ck", 512, 640, "kt", 2048)
+        for b in range(4):
+            quant("cd", 640 * b, 640 * b + 512, "bb", 3 - b)
+            quant("cd", 640 * b + 512, 640 * b + 640, "bb", 2048 + 3 - b)
+        ts(cols("tm", 0, C), dif, 0.0, 4096.0, A.is_equal, A.mult)
+        ts(dm, dif, 1.0, -1024.0, A.is_equal, A.mult)
+        tt(dm, dm, cols("tm", 0, C), A.add)
+
+    def table_constants():
+        ts(cn[8], p48, 16.0, None, A.mult)
+        ts(cn[9], p48, 14.0, None, A.mult)
+        ts(cn[10], p64, 1.0, -2.0, A.is_ge, A.add)
+        ts(cols("lc", 0, C), cols("lc", 0, C), cn[9], None, A.add)
+        fill(cols("lw", 0, 256), 0.0)
+        fill(cols("tw", 0, 256), 0.0)
+        for k in range(2):
+            zeros(cols("win", 448 * k, 448 * k + 448))
+        ts(cols("hb", 0, 1), cols("ii", 0, 1), 4, 1, A.logical_shift_right, A.bitwise_and)
+        fill(cols("qd", 0, 680), 0.0)
+        for k in range(2):
+            zeros(cols("ad", 448 * k, 448 * k + 448))
+        ts(cols("nz", 0, 32), cols("jm", 0, 32), pi, None, A.is_equal)
+        ts(cols("hn", 0, 32), cols("hn", 0, 32), p64, None, A.is_equal)
+        for t in range(2):
+            tt(cols("ad", 384 + t, 512, 4), cols("nz", 0, 32), cols("hn", 0, 32), A.mult)
+        ts(cols("ad", 386, 512, 4), cols("ad", 384, 512, 4), cn[8], None, A.mult)
+        quant("ca", 0, C, "ad", 0)
+        zeros(cols("et", 448, 512))
+        zeros(cols("zt", 0, 512))
+        quant("zq", 0, 128, "zt", 0)
+        for r in range(R):
+            for n, i in (("", 0), ("s", 1)):
+                o, z = T["lq%d%s" % (r, n)][:, K:128], T["zq" + n][:, 0:16]
+                if not i:
+                    o, z = o.bitcast(dt.uint8), z.bitcast(dt.uint8)
+                run("y", lambda: g.sync.dma_start(o, z), [cols("zq" + n, 0, 16)], [cols("lq%d%s" % (r, n), K, 128)], "dz", 16)
+        ts(cols("wo", 0, 128), cols("wi", 0, 128), pi, None, A.add)
+
+    def slot(tile, t, lo=0, hi=C):
+        return cols("ct", 896 * tile + t + 4 * lo, 896 * tile + 4 * hi, 4)
+
+    def listed(out, row, k):
+        scan(cols("scl", 0, C), dm, row, 0.0, A.add, A.min)
+        ts(out, cols("scl", 15, C, 16), k, None, A.add)
+
+    def entries(z, tmp, bank):
+        tt(cols(tmp, 0, C), ps(bank), wz, A.max)
+        scan(cols(z, 0, C), dz, cols(tmp, 0, C), BIG, A.max, A.min)
+
+    def own(z, bank, tile):
+        for c in range(14):
+            a = cols(z, 16 * c + 15, 16 * c + 16)
+            m = 16 * c + 16
+            if m < C:
+                ts(slot(tile + c // 4, c % 4, m, C), ps(bank, m, C), a, None, A.is_le)
+            ts(slot(tile + c // 4, c % 4, 0, m), ps(bank, 0, m), a, None, A.is_lt)
+            if c == 13:
+                tt(slot(tile + 3, 2), ps(bank), cols(z, 0, C), A.is_equal)
+            if c in (3, 7, 11, 13):
+                k = tile + c // 4
+                quant("qc", C * k, C * k + C, "ct", 896 * k)
+
+    def summed(k, col, last=False):
+        quant("qc", C * k, C * k + C, "ct", 896 * k)
+        mm(7, C, "ck", col, "qc", C * k, False, last)
+
+    for r in range(R):
+        quant("qx", 0, C, "xt", 0)
+        for k in range(5):
+            mm(k, C, "up", 128 * k, "qx", 0)
+        entries("z1", "tm", 0)
+        entries("z0", "tn", 1)
+        if r == 0:
+            later_constants()
+        act(cols("ab", 0, 14), cols("z0", 15, C, 16), AF.Abs)
+        for m in range(3):
+            act(cols("wm", 16 * m, 16 * m + 14), cols("ab", 0, 14), AF.Identity, bias=cn[3 + 2 * m], scale=cn[2 + 2 * m])
+        own("z1", 0, 0)
+        for m in (2, 0, 1):
+            tt(cols("lm", 16 * m, 16 * m + 14), cols("z0", 15, C, 16), cols("wm", 16 * m, 16 * m + 14), A.add if m == 2 else A.subtract)
+        if r == 0:
+            decode_constants()
+        k = 0
+        for b in range(4):
+            for s in range(5):
+                mm(5 + k % 2, C, "cd", 640 * b + 128 * s, "qx", 0)
+                if s:
+                    act(cols("fw", 896 * b + C * (s - 1), 896 * b + C * s), ps(5 + k % 2), AF.Copy, scale=0.5)
+                else:
+                    act(cols("fn", C * b, C * b + C), ps(5 + k % 2), AF.Copy)
+                k += 1
+        for k in range(4):
+            mm(0, C, "ck", 0, "qc", C * k, k == 0, k == 3)
+        mm(5, C, "up", 384, "qx", 0)
+        todo = [(15 + c // 4, c % 4, 4, c) for c in range(14)] + [(12, c, 5, c) for c in range(NS)]
+        for i in range(len(todo) + 1):
+            if i < len(todo):
+                tile, t, bank, c = todo[i]
+                act(cols("sg", C * (i % 4), C * (i % 4) + C), ps(bank), AF.Sign, bias=cols("lm", 32 + c, 33 + c), scale=-1.0)
+            if i:
+                tile, t, bank, c = todo[i - 1]
+                act(slot(tile, t), cols("sg", C * ((i - 1) % 4), C * ((i - 1) % 4) + C), AF.Relu)
+        own("z0", 1, 4)
+        if r == 0:
+            table_constants()
+        for k in range(4):
+            mm(1, C, "ck", 0, "qc", C * (4 + k), k == 0, k == 3)
+        for k in range(4):
+            mm(7, C, "ck", 0, "qc", C * (4 + k), k == 0, False)
+        listed(cols("l1", 0, 14), ps(0), kp)
+        sca(cols("lw", 0, 256), cols("l1", 0, 14), cols("lc", 0, C))
+        run("y", lambda: g.sync.dma_start(T.ld[:, :], T.lw[0:128:16, 0:256]), [cols("lw", 0, 256)], [(None, "ld", 0, 1024, 1)], "ld%d" % r, 16)
+        run("g", lambda: g.indirect_dma_start(out=T.lt[:, :], out_offset=None, in_=T.ld[:], in_offset=IndirectOffsetOnAxis(ap=T.hb[:, 0:1], axis=0), bounds_check=1),
+            [(None, "ld", 0, 1024, 1), cols("hb", 0, 1)], [cols("lt", 0, 1024)], "lt%d" % r, 16)
+        for c in range(14):
+            ts(slot(8 + c // 4, c % 4), ps(2), cols("lm", c, c + 1), None, A.is_le)
+            if c % 4 == 3:
+                summed(8 + c // 4, 128)
+        listed(cols("l0", 0, 14), ps(1), kp)
+        act(cols("r0s", 0, C), ps(1), AF.Copy)
+        for c in list(range(12, 14)) + list(range(NS, 12)):
+            ts(slot(12 + c // 4, c % 4) if c < 12 else slot(11, c - 10), ps(3), cols("lm", 16 + c, 17 + c), None, A.is_le)
+            if c in (7, 11):
+                summed(12 + c // 4, 256)
+            if c == 13:
+                summed(11, 512)
+        for k in range(15, 19):
+            summed(k, 384)
+        summed(12, 256, True)
+        listed(cols("lp", 0, 14), ps(7), kpm)
+        sca(cols("win", 0, 896), cols("lp", 0, 14), cols("r0s", 0, C))
+        for t in range(4):
+            scan(cols("sc", C * t, C * t + C), dm, cols("win", t, 896, 4), 0.0, A.add, A.min)
+        ts(cols("v56", 0, 56), cols("sc", 15, 896, 16), kp, None, A.add)
+        ts(cols("qd", 1, 224, 4), cols("v56", 0, 56), 1.5 * 2.0 ** 27, 1.5 * 2.0 ** 27, A.add, A.subtract)
+        ts(cols("qd", 2, 224, 4), cols("v56", 0, 56), 0.5, None, A.is_ge)
+        tt(cols("qd", 0, 224, 4), cols("v56", 0, 56), cols("qd", 1, 224, 4), A.subtract)
+        quant("qq", 0, 170, "qd", 0)
+        for m in range(4):
+            mm(0, 128, "ca", 96 - 32 * m, "qq", 14 * m, m == 0, m == 3)
+        act(cols("p0s", 0, C), ps(7), AF.Copy)
+        cp(cols("ei", 0, 14), ps(0, 0, 14))
+        gat(cols("pl", 0, C), cols("lt", 0, 1024), cols("ei", 0, 14))
+        scan(cols("sce", 0, C), dm, cols("pl", 0, C), 0.0, A.add, A.min)
+        ts(cols("eo", 0, 7), cols("sce", 15, K, 16), kp, None, A.add)
+        ts(cols("eo", 8, 15), cols("sce", K + 15, C, 16), kp, None, A.add)
+        for t in range(4):
+            sgat(cols("g1", K * t, K * t + K), cols("fw", 896 * t, 896 * t + 896), cols("eo", 0, 7))
+        for t in range(4):
+            gadd(cols("et", t, 448, 4), cols("fw", 896 * t, 896 * t + 896), cols("eo", 8, 15), cols("g1", K * t, K * t + K))
+        qe, lq = "qe%d" % r, "lq%d" % r
+        quant(qe, 0, 128, "et", 0)
+        rid, pid = topo.addr(nxt, core)
+        eng = topo.engines(core, nxt)[:8]
+        mask = sum(1 << e for e in eng)
+        total["snt%d" % r] = 2 * len(eng)
+        total["arr%d" % r] = 2 * len(eng)
+        for n in ("", "s"):
+            o, i = T[lq + n][:, 0:K], T[qe + n][:, 0:K]
+            if not n:
+                o, i = o.bitcast(dt.uint8), i.bitcast(dt.uint8)
+            run("g", lambda: g.remote_dma(out_ap=o, in_ap=i, remote_sem=T.sem["arr%d" % r], local_sem=T.sem["snt%d" % r], pid=pid, routing_id=rid, dma_engine_mask=mask),
+                [cols(qe + n, 0, K)], [], "snt%d" % r, 0)
+            acc.setdefault(lq + n, []).append((True, "arr%d" % r, 0, K, 1, 0))
+        sca(cols("tw", 0, 256), cols("l0", 0, 14), cols("p0s", 0, C))
+        gat(cols("pr", 0, C), cols("tw", 0, 256), cols("l1", 0, 14))
+        scan(cols("scx", 0, C), dm, cols("pr", 0, C), 0.0, A.add, A.min)
+        px, pa, pb, pg = [cols(n, 0, 14) for n in ("px", "pa", "pb", "pg")]
+        ts(px, cols("scx", 15, C, 16), kpm, None, A.add)
+        ts(pa, px, 3, None, A.bitwise_and)
+        ts(pb, px, 2, None, A.logical_shift_right)
+        ts(pg, pb, float(K), -float(K), A.is_ge, A.mult)
+        ts(pa, pa, float(K), None, A.mult)
+        tt(pb, pb, pg, A.add)
+        tt(cols("xo", 0, 14), pa, pb, A.add)
+        if r == 0:
+            codes(cols("wp", 0, 2048), cols("wa", 0, 512), cols("wo", 0, 128))
+            sgat(cols("wps", 0, 2048), cols("was", 0, 512), cols("wo", 0, 128))
+            quant("qv", 0, 128, "vt", 0)
+        if r < R - 1:
+            fill(cols("win", 0, 896), 0.0)
+        else:
+            act(cols("opb", 0, C), cols("pr", 0, C), AF.Identity, bias=cn[10], scale=2.0)
+            store("dop", T.op[:, :], T.opb[0:128:16, :], "opb", C)
+        for b in range(4):
+            for m in range(4):
+                k = 4 * b + m
+                mm(k % 8, 128, "wp", 128 * k, lq, 0)
+                o = cols("hw", 448 * b + K * m, 448 * b + K * m + K)
+                if m < 2:
+                    act(o, ps(k % 8, 0, K), AF.Copy, scale=0.015625)
+                else:
+                    ts(o, ps(k % 8, 0, K), 0.015625, None, A.mult)
+            gadd(cols("xt", b, 896, 4), cols("hw", 448 * b, 448 * b + 448), cols("xo", 0, 14), cols("fn", C * b, C * b + C))
+    quant("qx", 0, C, "xt", 0)
+    mm(0, C, "qv", 0, "qx", 0)
+    store("doc", T.oc[:, :], T.qx[:, :].bitcast(dt.uint8), "qx", C)
+    for k in range(4):
+        store("dos", T.osc[4 * k:4 * k + 4, :], T.qxs[32 * k:32 * k + 4, :], "qxs", C)
+    act(cols("yb", 0, C), ps(0), AF.Copy)
+    store("dy", T.y[:, :], T.yb[:, :], "yb", C)
+    for s in total:
+        wait("g", s, total[s])

@@ -3,7 +3,7 @@ from concourse.mybir import dt, AluOpType, ActivationFunctionType
 
 A, AF = AluOpType, ActivationFunctionType
 C, K, R = 224, 112, 3
-NS = 4
+NS = (0, 0, 0)
 BIG = 1e25
 F8, U8 = "float8_e4m3fn_x4", "uint8"
 SCRATCH = {}
@@ -22,7 +22,7 @@ for _n, _c in (("ii", 2), ("bi", 8), ("ui", 40), ("wi", 128), ("hb", 2), ("px", 
 for _n, _c in (("uo", 40), ("wo", 128), ("l1", 16), ("l0", 16), ("lp", 16), ("ei", 16), ("eo", 16), ("xo", 16)):
     _b(_n, _c, "uint16")
 for _n, _c in (("xt", 896), ("ut", 512), ("vt", 512), ("on", 128), ("mb", 640), ("bb", 2568), ("bm", 512), ("kt", 2560), ("nz", 32), ("ad", 896),
-               ("ct", 19 * 896), ("sg", 4 * C), ("fw", 3584), ("fn", 896), ("qd", 680), ("g1", 448), ("et", 512), ("hw", 1792), ("zt", 512)):
+               ("ct", 19 * 896), ("fw", 3584), ("fn", 896), ("qd", 680), ("g1", 448), ("et", 512), ("hw", 1792), ("zt", 512)):
     _b(_n, _c, "bfloat16")
 for _n, _c in [("qx", C), ("qu", 128), ("up", 640), ("qv", 128), ("cd", 2560), ("ck", 640), ("ca", C), ("qc", 19 * C), ("qq", 170), ("wa", 512),
                ("wp", 2048), ("zq", 128)] + [(n + str(r), c) for r in range(R) for n, c in (("qe", 128), ("lq", 128))]:
@@ -208,29 +208,38 @@ def rank_program(g, core, T, topo):
     ts(wz, wz, BIG, None, A.subtract)
     ts(dz, jm, 0.0, 2 * BIG, A.is_equal, A.mult)
     ts(dz, dz, BIG, None, A.subtract)
-    for k in range(5):
-        zeros(cols("bb", 512 * k, 512 * k + 512))
-    zeros(cols("bb", 2560, 2568))
     quant("qu", 0, 128, "ut", 0)
     for lo, hi in ((0, 16), (16, 40)):
         codes(cols("up", 16 * lo, 16 * hi), cols("qu", 0, 128), cols("uo", lo, hi))
         sgat(cols("ups", 16 * lo, 16 * hi), cols("qus", 0, 128), cols("uo", lo, hi))
-    act(cols("bb", 3, 3 + 2560, 4), cols("mb", 0, 640), AF.Copy)
 
     def later_constants():
         for k, (b, op) in enumerate(((b0, A.is_ge), (b1, A.is_ge), (b1, A.is_lt))):
             ts(cn[2 + 2 * k], b, 1.0, 1.25 * 2.0 ** -24, op, A.mult)
             ts(cn[3 + 2 * k], b, 1.0, 2.0 ** -120, op, A.mult)
-        for k in (3, 7):
-            zeros(cols("ct", 896 * k + 3, 896 * k + 896, 4))
-        for t in (2, 3):
-            zeros(cols("ct", 896 * 18 + t, 896 * 19, 4))
+        for k in range(5):
+            zeros(cols("bb", 512 * k, 512 * k + 512))
+        zeros(cols("bb", 2560, 2568))
+        act(cols("bb", 3, 3 + 2560, 4), cols("mb", 0, 640), AF.Copy)
+        zeros(cols("ct", 896 * 3 + 3, 896 * 4, 4))
         ts(cols("bm", 0, 512), cols("rm", 0, 512), p16, None, A.is_equal)
         for t in range(4):
             act(cols("kt", t, 2048, 4), cols("bm", 0, 512), AF.Copy)
             act(cols("kt", 2048 + t, 2560, 4), cols("bm", 128 + 128 * (t // 2), 256 + 128 * (t // 2)), AF.Copy)
 
     def decode_constants():
+        zeros(cols("ct", 896 * 7 + 3, 896 * 8, 4))
+        for t in (2, 3):
+            zeros(cols("ct", 896 * 18 + t, 896 * 19, 4))
+        for n in ("win", "ad"):
+            for k in range(2):
+                zeros(cols(n, 448 * k, 448 * k + 448))
+        zeros(cols("et", 448, 512))
+        zeros(cols("zt", 0, 512))
+        zeros(cols("lw", 0, 256))
+        zeros(cols("tw", 0, 256))
+        for k in range(2):
+            zeros(cols("qd", 340 * k, 340 * k + 340))
         quant("ck", 0, 512, "kt", 0)
         quant("ck", 512, 640, "kt", 2048)
         for b in range(4):
@@ -245,22 +254,13 @@ def rank_program(g, core, T, topo):
         ts(cn[9], p48, 14.0, None, A.mult)
         ts(cn[10], p64, 1.0, -2.0, A.is_ge, A.add)
         ts(cols("lc", 0, C), cols("lc", 0, C), cn[9], None, A.add)
-        fill(cols("lw", 0, 256), 0.0)
-        fill(cols("tw", 0, 256), 0.0)
-        for k in range(2):
-            zeros(cols("win", 448 * k, 448 * k + 448))
         ts(cols("hb", 0, 1), cols("ii", 0, 1), 4, 1, A.logical_shift_right, A.bitwise_and)
-        fill(cols("qd", 0, 680), 0.0)
-        for k in range(2):
-            zeros(cols("ad", 448 * k, 448 * k + 448))
         ts(cols("nz", 0, 32), cols("jm", 0, 32), pi, None, A.is_equal)
         ts(cols("hn", 0, 32), cols("hn", 0, 32), p64, None, A.is_equal)
         for t in range(2):
             tt(cols("ad", 384 + t, 512, 4), cols("nz", 0, 32), cols("hn", 0, 32), A.mult)
         ts(cols("ad", 386, 512, 4), cols("ad", 384, 512, 4), cn[8], None, A.mult)
         quant("ca", 0, C, "ad", 0)
-        zeros(cols("et", 448, 512))
-        zeros(cols("zt", 0, 512))
         quant("zq", 0, 128, "zt", 0)
         for r in range(R):
             for n, i in (("", 0), ("s", 1)):
@@ -299,6 +299,7 @@ def rank_program(g, core, T, topo):
         mm(7, C, "ck", col, "qc", C * k, False, last)
 
     for r in range(R):
+        ns = NS[r]
         quant("qx", 0, C, "xt", 0)
         for k in range(5):
             mm(k, C, "up", 128 * k, "qx", 0)
@@ -316,24 +317,21 @@ def rank_program(g, core, T, topo):
             decode_constants()
         k = 0
         for b in range(4):
-            for s in range(5):
-                mm(5 + k % 2, C, "cd", 640 * b + 128 * s, "qx", 0)
-                if s:
-                    act(cols("fw", 896 * b + C * (s - 1), 896 * b + C * s), ps(5 + k % 2), AF.Copy, scale=0.5)
-                else:
-                    act(cols("fn", C * b, C * b + C), ps(5 + k % 2), AF.Copy)
+            for s in range(4):
+                mm(5 + k % 2, C, "cd", 640 * b + 128 * s + 128, "qx", 0)
+                act(cols("fw", 896 * b + C * s, 896 * b + C * s + C), ps(5 + k % 2), AF.Copy, scale=0.5)
                 k += 1
         for k in range(4):
             mm(0, C, "ck", 0, "qc", C * k, k == 0, k == 3)
-        mm(5, C, "up", 384, "qx", 0)
-        todo = [(15 + c // 4, c % 4, 4, c) for c in range(14)] + [(12, c, 5, c) for c in range(NS)]
-        for i in range(len(todo) + 1):
-            if i < len(todo):
-                tile, t, bank, c = todo[i]
-                act(cols("sg", C * (i % 4), C * (i % 4) + C), ps(bank), AF.Sign, bias=cols("lm", 32 + c, 33 + c), scale=-1.0)
-            if i:
-                tile, t, bank, c = todo[i - 1]
-                act(slot(tile, t), cols("sg", C * ((i - 1) % 4), C * ((i - 1) % 4) + C), AF.Relu)
+        if ns:
+            mm(5, C, "up", 384, "qx", 0)
+        todo = [(15 + c // 4, c % 4, 4, c) for c in range(14)] + [(12 + c // 4, c % 4, 5, c) for c in range(ns)]
+        for tile, t, bank, c in todo:
+            act(slot(tile, t), ps(bank), AF.Sign, bias=cols("lm", 32 + c, 33 + c), scale=-1.0)
+            if t == 3:
+                act(cols("ct", 896 * tile, 896 * tile + 896), cols("ct", 896 * tile, 896 * tile + 896), AF.Relu)
+            elif tile == 18:
+                act(slot(tile, t), slot(tile, t), AF.Relu)
         own("z0", 1, 4)
         if r == 0:
             table_constants()
@@ -352,15 +350,16 @@ def rank_program(g, core, T, topo):
                 summed(8 + c // 4, 128)
         listed(cols("l0", 0, 14), ps(1), kp)
         act(cols("r0s", 0, C), ps(1), AF.Copy)
-        for c in list(range(12, 14)) + list(range(NS, 12)):
+        for c in range(13, ns - 1, -1):
             ts(slot(12 + c // 4, c % 4) if c < 12 else slot(11, c - 10), ps(3), cols("lm", 16 + c, 17 + c), None, A.is_le)
-            if c in (7, 11):
-                summed(12 + c // 4, 256)
-            if c == 13:
+            if c == 12:
                 summed(11, 512)
+            if c in (4, 8) or (c == 0 and not ns):
+                summed(12 + c // 4, 256)
         for k in range(15, 19):
-            summed(k, 384)
-        summed(12, 256, True)
+            summed(k, 384, k == 18 and not ns)
+        for k in range(ns // 4 - 1, -1, -1):
+            summed(12 + k, 256, not k)
         listed(cols("lp", 0, 14), ps(7), kpm)
         sca(cols("win", 0, 896), cols("lp", 0, 14), cols("r0s", 0, C))
         for t in range(4):
@@ -396,6 +395,9 @@ def rank_program(g, core, T, topo):
             run("g", lambda: g.remote_dma(out_ap=o, in_ap=i, remote_sem=T.sem["arr%d" % r], local_sem=T.sem["snt%d" % r], pid=pid, routing_id=rid, dma_engine_mask=mask),
                 [cols(qe + n, 0, K)], [], "snt%d" % r, 0)
             acc.setdefault(lq + n, []).append((True, "arr%d" % r, 0, K, 1, 0))
+        for b in range(4):
+            mm(1 + b, C, "cd", 640 * b, "qx", 0)
+            act(cols("fn", C * b, C * b + C), ps(1 + b), AF.Copy)
         sca(cols("tw", 0, 256), cols("l0", 0, 14), cols("p0s", 0, C))
         gat(cols("pr", 0, C), cols("tw", 0, 256), cols("l1", 0, 14))
         scan(cols("scx", 0, C), dm, cols("pr", 0, C), 0.0, A.add, A.min)
@@ -412,7 +414,8 @@ def rank_program(g, core, T, topo):
             sgat(cols("wps", 0, 2048), cols("was", 0, 512), cols("wo", 0, 128))
             quant("qv", 0, 128, "vt", 0)
         if r < R - 1:
-            fill(cols("win", 0, 896), 0.0)
+            for k in range(2):
+                zeros(cols("win", 448 * k, 448 * k + 448))
         else:
             act(cols("opb", 0, C), cols("pr", 0, C), AF.Identity, bias=cn[10], scale=2.0)
             store("dop", T.op[:, :], T.opb[0:128:16, :], "opb", C)

@@ -3,7 +3,8 @@ from concourse.mybir import dt, AluOpType, ActivationFunctionType
 
 A, AF = AluOpType, ActivationFunctionType
 C, K, R = 224, 112, 3
-NS = (0, 0, 0)
+NS = (4, 8, 8)
+FE = (10, 8, 8)
 BIG = 1e25
 F8, U8 = "float8_e4m3fn_x4", "uint8"
 SCRATCH = {}
@@ -14,15 +15,16 @@ def _b(name, cols, dtype="float32", where="sbuf"):
 
 
 for _n, _c in (("bf", 8), ("cn", 16), ("jm", C), ("dif", C), ("wz", C), ("dz", C), ("dm", C), ("tm", C), ("tn", C), ("lc", C), ("hn", 32), ("rm", 512),
-               ("z1", C), ("z0", C), ("ab", 16), ("wm", 48), ("lm", 48), ("scl", C), ("lw", 256), ("lt", 1024), ("r0s", C), ("p0s", C), ("win", 896),
-               ("sc", 896), ("v56", 56), ("pl", C), ("sce", C), ("tw", 256), ("pr", C), ("scx", C), ("opb", C), ("yb", C)):
+               ("z1", C), ("z0", C), ("ab", 16), ("wm", 48), ("lm", 48), ("scl", C), ("lw", 256), ("lt", 1024), ("p0s", C),
+               ("v56", 56), ("pl", C), ("sce", C), ("tw", 256), ("pr", C), ("scx", C), ("opb", C), ("yb", C)):
     _b(_n, _c)
 for _n, _c in (("ii", 2), ("bi", 8), ("ui", 40), ("wi", 128), ("hb", 2), ("px", 16), ("pa", 16), ("pb", 16), ("pg", 16)):
     _b(_n, _c, "int32")
 for _n, _c in (("uo", 40), ("wo", 128), ("l1", 16), ("l0", 16), ("lp", 16), ("ei", 16), ("eo", 16), ("xo", 16)):
     _b(_n, _c, "uint16")
 for _n, _c in (("xt", 896), ("ut", 512), ("vt", 512), ("on", 128), ("mb", 640), ("bb", 2568), ("bm", 512), ("kt", 2560), ("nz", 32), ("ad", 896),
-               ("ct", 19 * 896), ("fw", 3584), ("fn", 896), ("qd", 680), ("g1", 448), ("et", 512), ("hw", 1792), ("zt", 512)):
+               ("ct", 19 * 896), ("fw", 3584), ("fn", 896), ("qd", 680), ("g1", 448), ("et", 512), ("hw", 1792), ("zt", 512),
+               ("r0s", C), ("win", 896), ("sc", 896), ("db", C)):
     _b(_n, _c, "bfloat16")
 for _n, _c in [("qx", C), ("qu", 128), ("up", 640), ("qv", 128), ("cd", 2560), ("ck", 640), ("ca", C), ("qc", 19 * C), ("qq", 170), ("wa", 512),
                ("wp", 2048), ("zq", 128)] + [(n + str(r), c) for r in range(R) for n, c in (("qe", 128), ("lq", 128))]:
@@ -202,7 +204,7 @@ def rank_program(g, core, T, topo):
     kp, kpm = cn[0], cn[1]
     ts(kp, pi, 15.0, 1024.0, A.is_lt, A.mult)
     ts(kpm, kp, 1.0, None, A.subtract)
-    dif, wz, dz, dm, jm = [cols(n, 0, C) for n in ("dif", "wz", "dz", "dm", "jm")]
+    dif, wz, dz, dm, jm, db = [cols(n, 0, C) for n in ("dif", "wz", "dz", "dm", "jm", "db")]
     ts(dif, jm, pi, None, A.subtract)
     ts(wz, dif, 0.0, 2 * BIG, A.not_equal, A.mult)
     ts(wz, wz, BIG, None, A.subtract)
@@ -248,6 +250,8 @@ def rank_program(g, core, T, topo):
         ts(cols("tm", 0, C), dif, 0.0, 4096.0, A.is_equal, A.mult)
         ts(dm, dif, 1.0, -1024.0, A.is_equal, A.mult)
         tt(dm, dm, cols("tm", 0, C), A.add)
+        ts(db, dm, 0.25, None, A.mult)
+        ts(cn[11], kp, 0.25, None, A.mult)
 
     def table_constants():
         ts(cn[8], p48, 16.0, None, A.mult)
@@ -298,6 +302,12 @@ def rank_program(g, core, T, topo):
         quant("qc", C * k, C * k + C, "ct", 896 * k)
         mm(7, C, "ck", col, "qc", C * k, False, last)
 
+    def unpack(k0, k1, banks):
+        for k in range(k0, k1):
+            bank = banks[k % len(banks)]
+            mm(bank, C, "cd", 640 * (k // 4) + 128 * (k % 4) + 128, "qx", 0)
+            act(cols("fw", C * k, C * k + C), ps(bank), AF.Copy, scale=0.5)
+
     for r in range(R):
         ns = NS[r]
         quant("qx", 0, C, "xt", 0)
@@ -315,12 +325,7 @@ def rank_program(g, core, T, topo):
             tt(cols("lm", 16 * m, 16 * m + 14), cols("z0", 15, C, 16), cols("wm", 16 * m, 16 * m + 14), A.add if m == 2 else A.subtract)
         if r == 0:
             decode_constants()
-        k = 0
-        for b in range(4):
-            for s in range(4):
-                mm(5 + k % 2, C, "cd", 640 * b + 128 * s + 128, "qx", 0)
-                act(cols("fw", 896 * b + C * s, 896 * b + C * s + C), ps(5 + k % 2), AF.Copy, scale=0.5)
-                k += 1
+        unpack(0, FE[r], (5, 6))
         for k in range(4):
             mm(0, C, "ck", 0, "qc", C * k, k == 0, k == 3)
         if ns:
@@ -360,18 +365,18 @@ def rank_program(g, core, T, topo):
             summed(k, 384, k == 18 and not ns)
         for k in range(ns // 4 - 1, -1, -1):
             summed(12 + k, 256, not k)
+        unpack(FE[r], 16, (2, 3, 4, 5, 6))
         listed(cols("lp", 0, 14), ps(7), kpm)
         sca(cols("win", 0, 896), cols("lp", 0, 14), cols("r0s", 0, C))
         for t in range(4):
-            scan(cols("sc", C * t, C * t + C), dm, cols("win", t, 896, 4), 0.0, A.add, A.min)
-        ts(cols("v56", 0, 56), cols("sc", 15, 896, 16), kp, None, A.add)
+            scan(cols("sc", C * t, C * t + C), db, cols("win", t, 896, 4), 0.0, A.add, A.min)
+        ts(cols("v56", 0, 56), cols("sc", 15, 896, 16), cn[11], None, A.add)
         ts(cols("qd", 1, 224, 4), cols("v56", 0, 56), 1.5 * 2.0 ** 27, 1.5 * 2.0 ** 27, A.add, A.subtract)
         ts(cols("qd", 2, 224, 4), cols("v56", 0, 56), 0.5, None, A.is_ge)
         tt(cols("qd", 0, 224, 4), cols("v56", 0, 56), cols("qd", 1, 224, 4), A.subtract)
         quant("qq", 0, 170, "qd", 0)
         for m in range(4):
             mm(0, 128, "ca", 96 - 32 * m, "qq", 14 * m, m == 0, m == 3)
-        act(cols("p0s", 0, C), ps(7), AF.Copy)
         cp(cols("ei", 0, 14), ps(0, 0, 14))
         gat(cols("pl", 0, C), cols("lt", 0, 1024), cols("ei", 0, 14))
         scan(cols("sce", 0, C), dm, cols("pl", 0, C), 0.0, A.add, A.min)
@@ -395,6 +400,7 @@ def rank_program(g, core, T, topo):
             run("g", lambda: g.remote_dma(out_ap=o, in_ap=i, remote_sem=T.sem["arr%d" % r], local_sem=T.sem["snt%d" % r], pid=pid, routing_id=rid, dma_engine_mask=mask),
                 [cols(qe + n, 0, K)], [], "snt%d" % r, 0)
             acc.setdefault(lq + n, []).append((True, "arr%d" % r, 0, K, 1, 0))
+        act(cols("p0s", 0, C), ps(7), AF.Copy)
         for b in range(4):
             mm(1 + b, C, "cd", 640 * b, "qx", 0)
             act(cols("fn", C * b, C * b + C), ps(1 + b), AF.Copy)

from concourse.bass import IndirectOffsetOnAxis
from concourse.mybir import dt, AluOpType, ActivationFunctionType

A, AF = AluOpType, ActivationFunctionType
C, K, R = 224, 112, 3
NS = (4, 8, 8)
FE = (10, 8, 8)
BIG = 1e25
F8, U8 = "float8_e4m3fn_x4", "uint8"
SCRATCH = {}


def _b(name, cols, dtype="float32", where="sbuf"):
    SCRATCH[name] = (where, [128, cols], dtype)


for _n, _c in (("bf", 8), ("cn", 16), ("jm", C), ("dif", C), ("wz", C), ("dz", C), ("dm", C), ("tm", C), ("tn", C), ("lc", C), ("hn", 32), ("rm", 512),
               ("z1", C), ("z0", C), ("ab", 16), ("wm", 48), ("lm", 48), ("scl", C), ("lw", 256), ("lt", 1024), ("p0s", C),
               ("v56", 56), ("pl", C), ("sce", C), ("tw", 256), ("pr", C), ("scx", C), ("opb", C), ("yb", C)):
    _b(_n, _c)
for _n, _c in (("ii", 2), ("bi", 8), ("ui", 40), ("wi", 128), ("hb", 2), ("px", 16), ("pa", 16), ("pb", 16), ("pg", 16)):
    _b(_n, _c, "int32")
for _n, _c in (("uo", 40), ("wo", 128), ("l1", 16), ("l0", 16), ("lp", 16), ("ei", 16), ("eo", 16), ("xo", 16)):
    _b(_n, _c, "uint16")
for _n, _c in (("xt", 896), ("ut", 512), ("vt", 512), ("on", 128), ("mb", 640), ("bb", 2568), ("bm", 512), ("kt", 2560), ("nz", 32), ("ad", 896),
               ("ct", 19 * 896), ("fw", 3584), ("fn", 896), ("qd", 680), ("g1", 448), ("et", 512), ("hw", 1792), ("zt", 512),
               ("r0s", C), ("win", 896), ("sc", 896), ("db", C)):
    _b(_n, _c, "bfloat16")
for _n, _c in [("qx", C), ("qu", 128), ("up", 640), ("qv", 128), ("cd", 2560), ("ck", 640), ("ca", C), ("qc", 19 * C), ("qq", 170), ("wa", 512),
               ("wp", 2048), ("zq", 128)] + [(n + str(r), c) for r in range(R) for n, c in (("qe", 128), ("lq", 128))]:
    _b(_n, _c, F8)
    _b(_n + "s", _c, U8)
_b("ps", 4096, "float32", "psum")
SCRATCH["ld"] = ("dram", [2, 1024], "float32")
SEMAPHORES = ["sv", "st", "ss", "sg", "dx", "du", "dv", "dw", "dz", "doc", "dos", "dop", "dy"] + [n + str(r) for r in range(R) for n in ("ld", "lt", "snt", "arr")]


def rank_program(g, core, T, topo):
    rank = T.rank_of(core)
    if rank is None:
        return
    nxt = T.cores[(rank + 1) % len(T.cores)]
    Q = {"v": g.vector, "t": g.tensor, "s": g.scalar, "g": g, "y": g.sync}
    ENG = {"v": "sv", "t": "st", "s": "ss", "g": "sg"}
    total, known, acc = {}, {q: {} for q in Q}, {}

    def cols(name, lo, hi, step=1):
        return (T[name][:, lo:hi:step], name, lo, hi, step)

    def clash(a, lo, hi, step, psum):
        if psum:
            return a[2] // 512 == lo // 512
        return a[2] < hi and lo < a[3] and not (step > 1 and a[4] == step and (a[2] - lo) % step)

    def wait(q, sem, val):
        if known[q].get(sem, 0) < val:
            Q[q].wait_ge(T.sem[sem], val)
            known[q][sem] = val

    def run(q, emit, reads, writes, sem=None, inc=1):
        s = sem or ENG[q]
        need = {}
        for w, views in ((False, reads), (True, writes)):
            for _, name, lo, hi, step in views:
                psum = name == "ps"
                for a in acc.get(name, []):
                    if not clash(a, lo, hi, step, psum):
                        continue
                    if a[1] == s and (psum or sem is not None):
                        continue
                    if not psum and not (w or a[0]):
                        continue
                    need[a[1]] = max(need.get(a[1], 0), a[5] if a[5] else total[a[1]])
        for k in need:
            wait(q, k, need[k])
        ins = emit()
        if inc:
            ins.then_inc(T.sem[s], inc)
            total[s] = total.get(s, 0) + inc
        at = total[s] if sem is None else 0
        for w, views in ((False, reads), (True, writes)):
            for _, name, lo, hi, step in views:
                L = acc.setdefault(name, [])
                if name == "ps":
                    L[:] = [a for a in L if a[2] // 512 != lo // 512 or (not w and a[1] != s)]
                else:
                    L[:] = [a for a in L if not ((w or (a[1] == s and not a[0])) and lo <= a[2] and a[3] <= hi
                                                 and (step == 1 or (a[4] == step and (a[2] - lo) % step == 0)))]
                L.append((w, s, lo, hi, step, at))

    V, S = g.vector, g.scalar

    def ind(win, off):
        return win[0].indirect(off[0])

    def ts(out, in0, s1, s2, op0, op1=None):
        rd = [in0] + [x for x in (s1, s2) if isinstance(x, tuple)]
        a1 = s1[0] if isinstance(s1, tuple) else s1
        a2 = s2[0] if isinstance(s2, tuple) else s2
        if op1 is None:
            run("v", lambda: V.tensor_scalar(out[0], in0[0], a1, a2, op0), rd, [out])
        else:
            run("v", lambda: V.tensor_scalar(out[0], in0[0], a1, a2, op0, op1), rd, [out])

    def tt(out, a, b, op):
        run("v", lambda: V.tensor_tensor(out[0], a[0], b[0], op), [a, b], [out])

    def cp(out, a):
        run("v", lambda: V.tensor_copy(out[0], a[0]), [a], [out])

    def fill(out, c):
        run("v", lambda: V.memset(out[0], c), [], [out])

    def scan(out, d0, d1, init, o0, o1):
        run("v", lambda: V.tensor_tensor_scan(out[0], d0[0], d1[0], init, o0, o1), [d0, d1], [out])

    def gat(out, win, off):
        run("v", lambda: V.tensor_copy(out[0], ind(win, off)), [win, off], [out])

    def gadd(out, win, off, a):
        run("v", lambda: V.tensor_tensor(out[0], ind(win, off), a[0], A.add), [win, off, a], [out])

    def sca(win, off, a):
        run("v", lambda: V.tensor_copy(ind(win, off), a[0]), [off, a], [win])

    def codes(out, win, off):
        run("v", lambda: V.tensor_copy(out[0].bitcast(dt.uint32), win[0].bitcast(dt.uint32).indirect(off[0])), [win, off], [out])

    def act(out, a, func, bias=None, scale=None):
        kw = {}
        if bias is not None:
            kw["bias"] = bias[0] if isinstance(bias, tuple) else bias
        if scale is not None:
            kw["scale"] = scale[0] if isinstance(scale, tuple) else scale
        rd = [a] + [x for x in (bias, scale) if isinstance(x, tuple)]
        run("s", lambda: S.activation(out[0], a[0], func, **kw), rd, [out])

    def sgat(out, win, off):
        run("s", lambda: S.activation(out[0], ind(win, off), AF.Copy), [win, off], [out])

    def zeros(out):
        n = (out[3] - out[2] + out[4] - 1) // out[4]
        act(out, cols("rm", 0, n), AF.Copy, scale=0.0)

    def quant(name, lo, hi, src, slo):
        o, p, i = cols(name, lo, hi), cols(name + "s", lo, hi), cols(src, slo, slo + 4 * (hi - lo))
        run("v", lambda: V.quantize_mx(o[0], p[0], i[0]), [i], [o, p])

    def mm(bank, n, ln, la, rn, ra, start=True, stop=True):
        o = cols("ps", 512 * bank, 512 * bank + n)
        a, b = cols(ln, la, la + 128), cols(ln + "s", la, la + 128)
        c, d = cols(rn, ra, ra + n), cols(rn + "s", ra, ra + n)
        run("t", lambda: g.tensor.matmul_mx(o[0], a[0], b[0], c[0], d[0], start, stop), [a, b, c, d], [o])

    def ps(bank, lo=0, hi=C):
        return cols("ps", 512 * bank + lo, 512 * bank + hi)

    def load(sem, out, src, name, hi):
        run("y", lambda: g.sync.dma_start(out, src), [], [(None, name, 0, hi, 1)], sem, 16)

    def store(sem, out, src, name, hi):
        run("y", lambda: g.sync.dma_start(out, src), [(None, name, 0, hi, 1)], [], sem, 16)

    def iota(out, pattern, base, cm, flag=True):
        if flag:
            run("g", lambda: g.iota(out[0], pattern, base, cm, allow_small_or_imprecise_dtypes=True), [], [out])
        else:
            run("g", lambda: g.iota(out[0], pattern, base, cm), [], [out])

    load("du", T.ut[:, :], T.u[:, :], "ut", 512)
    load("dx", T.xt[:, :], T.x[:, :], "xt", 896)
    load("dw", T.wa[:, :].bitcast(dt.uint8), T.wc[:, :], "wa", 512)
    load("dw", T.was[:, :], T.ws[:, :], "was", 512)
    load("dv", T.vt[:, :], T.v[:, :], "vt", 512)

    iota(cols("ii", 0, 1), [[0, 1]], 0, 1, False)
    for k, (pat, base) in enumerate((([[16, 8]], 1), ([[16, 8]], 0), ([[32, 4], [-16, 2]], 16), ([[64, 2], [-32, 2], [16, 2]], 32), ([[64, 2], [-32, 2], [-16, 2]], 48))):
        iota(cols("ui", 8 * k, 8 * k + 8), pat, base, 0, False)
    iota(cols("jm", 0, C), [[0, 14], [1, 16]], 0, 0)
    iota(cols("rm", 0, 128), [[16, 8], [0, 16]], 0, 0)
    iota(cols("rm", 128, 256), [[32, 4], [-16, 2], [0, 16]], 16, 0)
    for h in range(2):
        iota(cols("rm", 256 + 64 * h, 320 + 64 * h), [[-32, 2], [16, 2], [0, 16]], 64 * h + 32, 0)
        iota(cols("rm", 384 + 64 * h, 448 + 64 * h), [[-16, 4], [0, 16]], 64 * h + 48, 0)
    fill(cols("on", 0, 128), 1.0)

    def select(lo, pat, base):
        o, i = cols("mb", lo, lo + 128), cols("on", 0, 128)
        run("g", lambda: g.affine_select(o[0], i[0], pat, A.is_equal, 0.0, base, 1), [i], [o])

    select(0, [[-1, 128]], 0)
    for s in range(4):
        select(128 + 128 * s, [[0, 4], [-64, 2], [-1, 16]], -16 * s)
    iota(cols("lc", 0, C), [[1, C]], 0, 0)
    iota(cols("hn", 0, 32), [[64, 2], [0, 16]], 0, 0)
    iota(cols("wi", 0, 128), [[32, 16], [16, 2], [0, 4]], 0, 0, False)

    for k, bits in enumerate((15, 112, 16, 32, 64, 48)):
        ts(cols("bi", k, k + 1), cols("ii", 0, 1), bits, None, A.bitwise_and)
    cp(cols("bf", 0, 6), cols("bi", 0, 6))
    cp(cols("uo", 0, 40), cols("ui", 0, 40))
    pi, p16, b0, b1, p64, p48 = [cols("bf", k, k + 1) for k in range(6)]
    cn = [cols("cn", k, k + 1) for k in range(16)]
    kp, kpm = cn[0], cn[1]
    ts(kp, pi, 15.0, 1024.0, A.is_lt, A.mult)
    ts(kpm, kp, 1.0, None, A.subtract)
    dif, wz, dz, dm, jm, db = [cols(n, 0, C) for n in ("dif", "wz", "dz", "dm", "jm", "db")]
    ts(dif, jm, pi, None, A.subtract)
    ts(wz, dif, 0.0, 2 * BIG, A.not_equal, A.mult)
    ts(wz, wz, BIG, None, A.subtract)
    ts(dz, jm, 0.0, 2 * BIG, A.is_equal, A.mult)
    ts(dz, dz, BIG, None, A.subtract)
    quant("qu", 0, 128, "ut", 0)
    for lo, hi in ((0, 16), (16, 40)):
        codes(cols("up", 16 * lo, 16 * hi), cols("qu", 0, 128), cols("uo", lo, hi))
        sgat(cols("ups", 16 * lo, 16 * hi), cols("qus", 0, 128), cols("uo", lo, hi))

    def later_constants():
        for k, (b, op) in enumerate(((b0, A.is_ge), (b1, A.is_ge), (b1, A.is_lt))):
            ts(cn[2 + 2 * k], b, 1.0, 1.25 * 2.0 ** -24, op, A.mult)
            ts(cn[3 + 2 * k], b, 1.0, 2.0 ** -120, op, A.mult)
        for k in range(5):
            zeros(cols("bb", 512 * k, 512 * k + 512))
        zeros(cols("bb", 2560, 2568))
        act(cols("bb", 3, 3 + 2560, 4), cols("mb", 0, 640), AF.Copy)
        zeros(cols("ct", 896 * 3 + 3, 896 * 4, 4))
        ts(cols("bm", 0, 512), cols("rm", 0, 512), p16, None, A.is_equal)
        for t in range(4):
            act(cols("kt", t, 2048, 4), cols("bm", 0, 512), AF.Copy)
            act(cols("kt", 2048 + t, 2560, 4), cols("bm", 128 + 128 * (t // 2), 256 + 128 * (t // 2)), AF.Copy)

    def decode_constants():
        zeros(cols("ct", 896 * 7 + 3, 896 * 8, 4))
        for t in (2, 3):
            zeros(cols("ct", 896 * 18 + t, 896 * 19, 4))
        for n in ("win", "ad"):
            for k in range(2):
                zeros(cols(n, 448 * k, 448 * k + 448))
        zeros(cols("et", 448, 512))
        zeros(cols("zt", 0, 512))
        zeros(cols("lw", 0, 256))
        zeros(cols("tw", 0, 256))
        for k in range(2):
            zeros(cols("qd", 340 * k, 340 * k + 340))
        quant("ck", 0, 512, "kt", 0)
        quant("ck", 512, 640, "kt", 2048)
        for b in range(4):
            quant("cd", 640 * b, 640 * b + 512, "bb", 3 - b)
            quant("cd", 640 * b + 512, 640 * b + 640, "bb", 2048 + 3 - b)
        ts(cols("tm", 0, C), dif, 0.0, 4096.0, A.is_equal, A.mult)
        ts(dm, dif, 1.0, -1024.0, A.is_equal, A.mult)
        tt(dm, dm, cols("tm", 0, C), A.add)
        ts(db, dm, 0.25, None, A.mult)
        ts(cn[11], kp, 0.25, None, A.mult)

    def table_constants():
        ts(cn[8], p48, 16.0, None, A.mult)
        ts(cn[9], p48, 14.0, None, A.mult)
        ts(cn[10], p64, 1.0, -2.0, A.is_ge, A.add)
        ts(cols("lc", 0, C), cols("lc", 0, C), cn[9], None, A.add)
        ts(cols("hb", 0, 1), cols("ii", 0, 1), 4, 1, A.logical_shift_right, A.bitwise_and)
        ts(cols("nz", 0, 32), cols("jm", 0, 32), pi, None, A.is_equal)
        ts(cols("hn", 0, 32), cols("hn", 0, 32), p64, None, A.is_equal)
        for t in range(2):
            tt(cols("ad", 384 + t, 512, 4), cols("nz", 0, 32), cols("hn", 0, 32), A.mult)
        ts(cols("ad", 386, 512, 4), cols("ad", 384, 512, 4), cn[8], None, A.mult)
        quant("ca", 0, C, "ad", 0)
        quant("zq", 0, 128, "zt", 0)
        for r in range(R):
            for n, i in (("", 0), ("s", 1)):
                o, z = T["lq%d%s" % (r, n)][:, K:128], T["zq" + n][:, 0:16]
                if not i:
                    o, z = o.bitcast(dt.uint8), z.bitcast(dt.uint8)
                run("y", lambda: g.sync.dma_start(o, z), [cols("zq" + n, 0, 16)], [cols("lq%d%s" % (r, n), K, 128)], "dz", 16)
        ts(cols("wo", 0, 128), cols("wi", 0, 128), pi, None, A.add)

    def slot(tile, t, lo=0, hi=C):
        return cols("ct", 896 * tile + t + 4 * lo, 896 * tile + 4 * hi, 4)

    def listed(out, row, k):
        scan(cols("scl", 0, C), dm, row, 0.0, A.add, A.min)
        ts(out, cols("scl", 15, C, 16), k, None, A.add)

    def entries(z, tmp, bank):
        tt(cols(tmp, 0, C), ps(bank), wz, A.max)
        scan(cols(z, 0, C), dz, cols(tmp, 0, C), BIG, A.max, A.min)

    def own(z, bank, tile):
        for c in range(14):
            a = cols(z, 16 * c + 15, 16 * c + 16)
            m = 16 * c + 16
            if m < C:
                ts(slot(tile + c // 4, c % 4, m, C), ps(bank, m, C), a, None, A.is_le)
            ts(slot(tile + c // 4, c % 4, 0, m), ps(bank, 0, m), a, None, A.is_lt)
            if c == 13:
                tt(slot(tile + 3, 2), ps(bank), cols(z, 0, C), A.is_equal)
            if c in (3, 7, 11, 13):
                k = tile + c // 4
                quant("qc", C * k, C * k + C, "ct", 896 * k)

    def summed(k, col, last=False):
        quant("qc", C * k, C * k + C, "ct", 896 * k)
        mm(7, C, "ck", col, "qc", C * k, False, last)

    def unpack(k0, k1, banks):
        for k in range(k0, k1):
            bank = banks[k % len(banks)]
            mm(bank, C, "cd", 640 * (k // 4) + 128 * (k % 4) + 128, "qx", 0)
            act(cols("fw", C * k, C * k + C), ps(bank), AF.Copy, scale=0.5)

    for r in range(R):
        ns = NS[r]
        quant("qx", 0, C, "xt", 0)
        for k in range(5):
            mm(k, C, "up", 128 * k, "qx", 0)
        entries("z1", "tm", 0)
        entries("z0", "tn", 1)
        if r == 0:
            later_constants()
        act(cols("ab", 0, 14), cols("z0", 15, C, 16), AF.Abs)
        for m in range(3):
            act(cols("wm", 16 * m, 16 * m + 14), cols("ab", 0, 14), AF.Identity, bias=cn[3 + 2 * m], scale=cn[2 + 2 * m])
        own("z1", 0, 0)
        for m in (2, 0, 1):
            tt(cols("lm", 16 * m, 16 * m + 14), cols("z0", 15, C, 16), cols("wm", 16 * m, 16 * m + 14), A.add if m == 2 else A.subtract)
        if r == 0:
            decode_constants()
        unpack(0, FE[r], (5, 6))
        for k in range(4):
            mm(0, C, "ck", 0, "qc", C * k, k == 0, k == 3)
        if ns:
            mm(5, C, "up", 384, "qx", 0)
        todo = [(15 + c // 4, c % 4, 4, c) for c in range(14)] + [(12 + c // 4, c % 4, 5, c) for c in range(ns)]
        for tile, t, bank, c in todo:
            act(slot(tile, t), ps(bank), AF.Sign, bias=cols("lm", 32 + c, 33 + c), scale=-1.0)
            if t == 3:
                act(cols("ct", 896 * tile, 896 * tile + 896), cols("ct", 896 * tile, 896 * tile + 896), AF.Relu)
            elif tile == 18:
                act(slot(tile, t), slot(tile, t), AF.Relu)
        own("z0", 1, 4)
        if r == 0:
            table_constants()
        for k in range(4):
            mm(1, C, "ck", 0, "qc", C * (4 + k), k == 0, k == 3)
        for k in range(4):
            mm(7, C, "ck", 0, "qc", C * (4 + k), k == 0, False)
        listed(cols("l1", 0, 14), ps(0), kp)
        sca(cols("lw", 0, 256), cols("l1", 0, 14), cols("lc", 0, C))
        run("y", lambda: g.sync.dma_start(T.ld[:, :], T.lw[0:128:16, 0:256]), [cols("lw", 0, 256)], [(None, "ld", 0, 1024, 1)], "ld%d" % r, 16)
        run("g", lambda: g.indirect_dma_start(out=T.lt[:, :], out_offset=None, in_=T.ld[:], in_offset=IndirectOffsetOnAxis(ap=T.hb[:, 0:1], axis=0), bounds_check=1),
            [(None, "ld", 0, 1024, 1), cols("hb", 0, 1)], [cols("lt", 0, 1024)], "lt%d" % r, 16)
        for c in range(14):
            ts(slot(8 + c // 4, c % 4), ps(2), cols("lm", c, c + 1), None, A.is_le)
            if c % 4 == 3:
                summed(8 + c // 4, 128)
        listed(cols("l0", 0, 14), ps(1), kp)
        act(cols("r0s", 0, C), ps(1), AF.Copy)
        for c in range(13, ns - 1, -1):
            ts(slot(12 + c // 4, c % 4) if c < 12 else slot(11, c - 10), ps(3), cols("lm", 16 + c, 17 + c), None, A.is_le)
            if c == 12:
                summed(11, 512)
            if c in (4, 8) or (c == 0 and not ns):
                summed(12 + c // 4, 256)
        for k in range(15, 19):
            summed(k, 384, k == 18 and not ns)
        for k in range(ns // 4 - 1, -1, -1):
            summed(12 + k, 256, not k)
        unpack(FE[r], 16, (2, 3, 4, 5, 6))
        listed(cols("lp", 0, 14), ps(7), kpm)
        sca(cols("win", 0, 896), cols("lp", 0, 14), cols("r0s", 0, C))
        for t in range(4):
            scan(cols("sc", C * t, C * t + C), db, cols("win", t, 896, 4), 0.0, A.add, A.min)
        ts(cols("v56", 0, 56), cols("sc", 15, 896, 16), cn[11], None, A.add)
        ts(cols("qd", 1, 224, 4), cols("v56", 0, 56), 1.5 * 2.0 ** 27, 1.5 * 2.0 ** 27, A.add, A.subtract)
        ts(cols("qd", 2, 224, 4), cols("v56", 0, 56), 0.5, None, A.is_ge)
        tt(cols("qd", 0, 224, 4), cols("v56", 0, 56), cols("qd", 1, 224, 4), A.subtract)
        quant("qq", 0, 170, "qd", 0)
        for m in range(4):
            mm(0, 128, "ca", 96 - 32 * m, "qq", 14 * m, m == 0, m == 3)
        cp(cols("ei", 0, 14), ps(0, 0, 14))
        gat(cols("pl", 0, C), cols("lt", 0, 1024), cols("ei", 0, 14))
        scan(cols("sce", 0, C), dm, cols("pl", 0, C), 0.0, A.add, A.min)
        ts(cols("eo", 0, 7), cols("sce", 15, K, 16), kp, None, A.add)
        ts(cols("eo", 8, 15), cols("sce", K + 15, C, 16), kp, None, A.add)
        for t in range(4):
            sgat(cols("g1", K * t, K * t + K), cols("fw", 896 * t, 896 * t + 896), cols("eo", 0, 7))
        for t in range(4):
            gadd(cols("et", t, 448, 4), cols("fw", 896 * t, 896 * t + 896), cols("eo", 8, 15), cols("g1", K * t, K * t + K))
        qe, lq = "qe%d" % r, "lq%d" % r
        quant(qe, 0, 128, "et", 0)
        rid, pid = topo.addr(nxt, core)
        eng = topo.engines(core, nxt)[:8]
        mask = sum(1 << e for e in eng)
        total["snt%d" % r] = 2 * len(eng)
        total["arr%d" % r] = 2 * len(eng)
        for n in ("", "s"):
            o, i = T[lq + n][:, 0:K], T[qe + n][:, 0:K]
            if not n:
                o, i = o.bitcast(dt.uint8), i.bitcast(dt.uint8)
            run("g", lambda: g.remote_dma(out_ap=o, in_ap=i, remote_sem=T.sem["arr%d" % r], local_sem=T.sem["snt%d" % r], pid=pid, routing_id=rid, dma_engine_mask=mask),
                [cols(qe + n, 0, K)], [], "snt%d" % r, 0)
            acc.setdefault(lq + n, []).append((True, "arr%d" % r, 0, K, 1, 0))
        act(cols("p0s", 0, C), ps(7), AF.Copy)
        for b in range(4):
            mm(1 + b, C, "cd", 640 * b, "qx", 0)
            act(cols("fn", C * b, C * b + C), ps(1 + b), AF.Copy)
        sca(cols("tw", 0, 256), cols("l0", 0, 14), cols("p0s", 0, C))
        gat(cols("pr", 0, C), cols("tw", 0, 256), cols("l1", 0, 14))
        scan(cols("scx", 0, C), dm, cols("pr", 0, C), 0.0, A.add, A.min)
        px, pa, pb, pg = [cols(n, 0, 14) for n in ("px", "pa", "pb", "pg")]
        ts(px, cols("scx", 15, C, 16), kpm, None, A.add)
        ts(pa, px, 3, None, A.bitwise_and)
        ts(pb, px, 2, None, A.logical_shift_right)
        ts(pg, pb, float(K), -float(K), A.is_ge, A.mult)
        ts(pa, pa, float(K), None, A.mult)
        tt(pb, pb, pg, A.add)
        tt(cols("xo", 0, 14), pa, pb, A.add)
        if r == 0:
            codes(cols("wp", 0, 2048), cols("wa", 0, 512), cols("wo", 0, 128))
            sgat(cols("wps", 0, 2048), cols("was", 0, 512), cols("wo", 0, 128))
            quant("qv", 0, 128, "vt", 0)
        if r < R - 1:
            for k in range(2):
                zeros(cols("win", 448 * k, 448 * k + 448))
        else:
            act(cols("opb", 0, C), cols("pr", 0, C), AF.Identity, bias=cn[10], scale=2.0)
            store("dop", T.op[:, :], T.opb[0:128:16, :], "opb", C)
        for b in range(4):
            for m in range(4):
                k = 4 * b + m
                mm(k % 8, 128, "wp", 128 * k, lq, 0)
                o = cols("hw", 448 * b + K * m, 448 * b + K * m + K)
                if m < 2:
                    act(o, ps(k % 8, 0, K), AF.Copy, scale=0.015625)
                else:
                    ts(o, ps(k % 8, 0, K), 0.015625, None, A.mult)
            gadd(cols("xt", b, 896, 4), cols("hw", 448 * b, 448 * b + 448), cols("xo", 0, 14), cols("fn", C * b, C * b + C))
    quant("qx", 0, C, "xt", 0)
    mm(0, C, "qv", 0, "qx", 0)
    store("doc", T.oc[:, :], T.qx[:, :].bitcast(dt.uint8), "qx", C)
    for k in range(4):
        store("dos", T.osc[4 * k:4 * k + 4, :], T.qxs[32 * k:32 * k + 4, :], "qxs", C)
    act(cols("yb", 0, C), ps(0), AF.Copy)
    store("dy", T.y[:, :], T.yb[:, :], "yb", C)
    for s in total:
        wait("g", s, total[s])
